import numpy as np
import ml_dtypes


def mxq(x, axis, fmt="e4m3"):
    dtype, down = {"e4m3": (ml_dtypes.float8_e4m3fn, 7), "e5m2": (ml_dtypes.float8_e5m2, 14)}[fmt]
    v = np.moveaxis(np.asarray(x, np.float32).astype(ml_dtypes.bfloat16).astype(np.float64), axis, -1)
    blocks = v.reshape(v.shape[:-1] + (-1, 32))
    amax = np.abs(blocks).max(-1, keepdims=True)
    byte = np.maximum(np.where(amax > 0, np.frexp(amax)[1] - 1 + 127, 0) - down, 1)
    scale = np.exp2(byte - 127.0)
    codes = (blocks / scale).astype(np.float32).astype(dtype).astype(np.float64)
    return np.moveaxis((codes * scale).reshape(v.shape), -1, axis)


WIDE = False


def mx_kscale(k):
    if not WIDE:
        return np.ones(k)
    levels = np.array([10, -10, 5, -5, 0])
    if k % 512:
        return np.exp2(np.random.permutation(np.resize(levels, k // 32))).repeat(32)
    a = np.empty((k // 512, 16))
    for p in range(k // 512):
        a[p, :8] = np.random.permutation(np.resize(levels, 8))
        for g in range(8):
            far = levels[np.abs(levels - a[p, g]) >= 10]
            a[p, g + 8] = far[np.random.randint(len(far))]
    return np.exp2(a.ravel()).repeat(32)


def f64(x):
    return np.asarray(x).astype(np.float64)


def striped(idx):
    return np.tile(idx.reshape(-1, 16).T, (8, 1)).astype(np.uint16)


def unstriped(offs):
    return offs[:16].T.reshape(-1).astype(np.int64)


def silu(v):
    return v / (1.0 + np.exp(-np.maximum(v, -700.0)))


K, T, E, C, H, N = 512, 2048, 8, 256, 512, 128
TOP = 3
PAD = 64


def by_expert(wq, xq):
    return np.concatenate([wq[e].T @ xq[:, e * C:(e + 1) * C] for e in range(E)], axis=1)


def setup_inputs():
    n = np.random.standard_normal
    s = mx_kscale(K)[:, None]
    u = mx_kscale(H)
    slot_token = np.empty(E * C, np.int64); pos = np.tile(E * C + np.arange(T) % PAD, (TOP, 1)); taken = np.zeros(T, np.int64)
    liked = np.random.randn(T)
    for e in np.random.permutation(E):
        free = np.flatnonzero(taken < TOP); pick = np.random.permutation(free[np.argsort(-(liked[free] + np.random.gumbel(size=free.size)))[:C]]); slot_token[e * C:(e + 1) * C] = pick
        pos[taken[pick], pick] = e * C + np.arange(C); taken[pick] += 1
    g = np.random.uniform(0.2, 0.8, (TOP, T))
    return {
        "xT": (n((K, T)) * s).astype(np.float32),
        "w1": (n((E, K, H)) / np.sqrt(K) / s[None]).astype(np.float32),
        "w3": (n((E, K, H)) / np.sqrt(K) / s[None] * u[None, None, :]).astype(np.float32),
        "w2": (n((E, H, N)) / np.sqrt(H) / u[None, :, None]).astype(np.float32),
        "gate": np.stack([np.tile(r, (N, 1)) for r in g]).astype(np.float32),
        "offs": striped(slot_token),
        "pos1": striped(pos[0]),
        "pos2": striped(pos[1]),
        "pos3": striped(pos[2]),
    }


def reference(xT, w1, w3, w2, gate, offs, pos1, pos2, pos3):
    idx = unstriped(offs)
    xq = mxq(f64(xT)[:, idx], 0, "e4m3")
    h = silu(by_expert(mxq(f64(w1), 1, "e4m3"), xq))
    h = h * by_expert(mxq(f64(w3), 1, "e4m3"), xq)
    y = by_expert(mxq(f64(w2), 1, "e4m3"), mxq(h, 0, "e4m3"))
    y = np.concatenate([y, np.zeros((N, PAD))], axis=1)
    return sum(f64(gate[r]) * y[:, unstriped(p)] for r, p in enumerate((pos1, pos2, pos3)))

@@ -1,0 +1,246 @@
+from contextlib import ExitStack
+
+import concourse.mybir as mybir
+
+K, T, E, C, H, N = 512, 2048, 8, 256, 512, 128
+TOP = 3
+PAD = 64
+SLOTS = E * C
+FLOPS = 2 * SLOTS * (2 * K * H + H * N)
+
+F32 = mybir.dt.float32
+BF16 = mybir.dt.bfloat16
+U32 = mybir.dt.uint32
+U16 = mybir.dt.uint16
+U8 = mybir.dt.uint8
+FP8X4 = mybir.dt.float8_e4m3fn_x4
+COPY = mybir.ActivationFunctionType.Copy
+SILU = mybir.ActivationFunctionType.Silu
+MULT = mybir.AluOpType.mult
+ADD = mybir.AluOpType.add
+
+P = 128
+PACK = 4
+LIST_ROWS = 16
+X_CHUNK = 512
+HALF = 128
+W2_GROUP = 2
+GATHER_EXPERTS = 1
+RING = 16
+SLOT_BYTES = 8192
+GATHER_AFTER = [None, None, None, ("w1", 0), ("w3", 0), ("w1", 2), ("w1", 3), ("w1", 4)]
+SILU_AFTER = [("w1", e + 1) for e in range(E - 1)] + [None]
+V_W1 = [0, 0, 0, 0, 0, 0, 0, 0]
+V_W3 = [64, 96, 96, 96, 96, 128, 128, 64]
+V_X = 288
+V_W2 = [0, 0, 32, 32]
+OUT_CHUNKS = [512, 512, 512, 256, 256]
+
+
+def tile_moe_ecr_glu_silu_kernel(tc, xT, w1, w3, w2, gate, offs, pos1, pos2, pos3, out):
+    nc = tc.nc
+    with ExitStack() as ctx:
+        keep = ctx.enter_context(tc.tile_pool(name="keep", bufs=1))
+        raw_pool = ctx.enter_context(tc.tile_pool(name="raw", bufs=1))
+        bf_pool = ctx.enter_context(tc.tile_pool(name="bf", bufs=5))
+        code_pool = ctx.enter_context(tc.tile_pool(name="code", bufs=4))
+        act_pool = ctx.enter_context(tc.tile_pool(name="act", bufs=3))
+        tail_pool = ctx.enter_context(tc.tile_pool(name="tail", bufs=2))
+        psum = ctx.enter_context(tc.psum_pool(name="psum", bufs=3))
+
+        x_codes = keep.tile([P, T], U32, align_bytes=64)
+        x_scales = keep.tile([P, T], U8, align_bytes=64)
+        y_slots = keep.tile([P, SLOTS + PAD], F32, align_bytes=64)
+        zeros = keep.tile([P, PAD], F32)
+        nc.gpsimd.memset(zeros[:], 0.0)
+        nc.gpsimd.memset(x_scales[:], 0)
+        nc.scalar.activation(y_slots[:, SLOTS:], zeros[:], SILU)
+
+        loads = []
+
+        def ring_tile(shape, label):
+            slot = len(loads) % RING
+            loads.append(label)
+            return raw_pool.tile(shape, F32, name="raw%d" % slot, align_bytes=64, offset=slot * SLOT_BYTES)
+
+        def tenant(pool, shape, dtype, name, after, place):
+            if after is None:
+                return pool.tile(shape, dtype, name=name, align_bytes=64)
+            slot = loads.index(after) % RING
+            return raw_pool.tile(shape, dtype, name="%s_in%d" % (name, slot), align_bytes=64,
+                                 offset=slot * SLOT_BYTES + place)
+
+        def load_rows(rows, label):
+            raw = ring_tile([P, PACK, 512], label)
+            nc.sync.dma_start(raw[:], rows)
+            return raw
+
+        def round_split(dst, src, split, total):
+            if split > 0:
+                nc.vector.tensor_copy(dst[:, :split], src[:, :split])
+            if split < total:
+                nc.scalar.activation(dst[:, split:], src[:, split:], COPY)
+
+        def quantise(codes, scales, grouped):
+            nc.vector.quantize_mx(out=codes.bitcast(FP8X4), scales=scales, in_=grouped)
+
+        x_rows = xT.rearrange("(p j) t -> p j t", j=PACK)
+        x_raw = []
+        lists = {}
+        for c in range(T // X_CHUNK):
+            x_raw.append(load_rows(x_rows[:, :, c * X_CHUNK:(c + 1) * X_CHUNK], ("x", c)))
+            if c == 0:
+                lists["offs"] = keep.tile([P, SLOTS // LIST_ROWS], U16, name="offs_list")
+                nc.sync.dma_start(lists["offs"][:], offs)
+        x_bf = []
+        for c in range(T // X_CHUNK):
+            grouped = bf_pool.tile([P, 512 * PACK], BF16, name="grouped", align_bytes=64)
+            round_split(grouped[:].rearrange("p (c i j) -> p c j i", i=4, j=PACK),
+                        x_raw[c][:].rearrange("p j (c i) -> p c j i", i=4), V_X // 4, X_CHUNK // 4)
+            x_bf.append(grouped)
+            if c > 0:
+                cols = slice((c - 1) * X_CHUNK, c * X_CHUNK)
+                quantise(x_codes[:, cols], x_scales[:, cols], x_bf[c - 1][:])
+        cols = slice(T - X_CHUNK, T)
+        quantise(x_codes[:, cols], x_scales[:, cols], x_bf[-1][:])
+
+        slot_codes, slot_scales = {}, {}
+
+        def gather_tokens(g):
+            width = GATHER_EXPERTS * C
+            part = lists["offs"][:, g * width // LIST_ROWS:(g + 1) * width // LIST_ROWS]
+            codes = tenant(keep, [P, width], U32, "slot_codes%d" % g, GATHER_AFTER[g], 4096 + 1024 * (g % 2))
+            scales = tenant(keep, [P, width], U8, "slot_scales%d" % g, GATHER_AFTER[g], 6144 + 256 * (g % 2))
+            nc.vector.tensor_copy(codes[:], x_codes[:].indirect(part))
+            nc.vector.tensor_copy(scales[:], x_scales[:].indirect(part))
+            slot_codes[g], slot_scales[g] = codes, scales
+
+        def round_first(w, label, e, split):
+            raw = load_rows(w[e].rearrange("(p j) h -> p j h", j=PACK), (label, e))
+            grouped = bf_pool.tile([P, 512 * PACK], BF16, name="grouped", align_bytes=64)
+            round_split(grouped[:].rearrange("p (t m j) -> p m j t", t=PACK, j=PACK),
+                        raw[:].rearrange("p j (m t) -> p m j t", t=PACK), split, P)
+            return grouped
+
+        def quantise_weights(grouped):
+            codes = code_pool.tile([P, 512], U32, name="w_codes", align_bytes=64)
+            scales = code_pool.tile([P, 512], U8, name="w_scales", align_bytes=64)
+            quantise(codes[:], scales[:], grouped[:])
+            return codes, scales
+
+        def round_second(g):
+            raw = ring_tile([P, W2_GROUP, PACK, N], ("w2", g))
+            nc.sync.dma_start(raw[:].rearrange("p e j n -> p e (j n)"),
+                              w2[g * W2_GROUP:(g + 1) * W2_GROUP].rearrange("e (p j) n -> p e (j n)", j=PACK))
+            grouped = bf_pool.tile([P, W2_GROUP * N * PACK], BF16, name="grouped", align_bytes=64)
+            view = grouped[:].rearrange("p (e c i j) -> p e c j i", e=W2_GROUP, i=4, j=PACK)
+            for e in range(W2_GROUP):
+                split = min(max(V_W2[g] - e * N // 4, 0), N // 4)
+                round_split(view[:, e], raw[:, e].rearrange("p j (c i) -> p c j i", i=4), split, N // 4)
+            return grouped
+
+        def project(name, weights, e, half):
+            codes, scales = weights
+            g, first = divmod(e * C + half * HALF, GATHER_EXPERTS * C)
+            cols = slice(first, first + HALF)
+            bank = psum.tile([P, PACK, HALF], F32, name=name)
+            for t in range(PACK):
+                wcols = slice(t * P, (t + 1) * P)
+                nc.tensor.matmul_mx(out=bank[:, t, :], lhsT=codes[:, wcols].bitcast(FP8X4), lhsT_scale=scales[:, wcols],
+                                    rhs=slot_codes[g][:, cols].bitcast(FP8X4), rhs_scale=slot_scales[g][:, cols],
+                                    start=True, stop=True)
+            return bank
+
+        h_bf, h_mx, w2_mx = {}, {}, {}
+
+        def hidden_half(e, half):
+            if half == 0:
+                h_bf[e] = act_pool.tile([P, C, PACK], BF16, name="h", align_bytes=64)
+            a = project("a_bank", q1[e], e, half)
+            b = project("b_bank", q3[e], e, half)
+            s = tenant(keep, [P, HALF, PACK], F32, "silu%d" % half, SILU_AFTER[e], 2048 * half)
+            nc.scalar.activation(s[:], a[:].rearrange("p t n -> p n t"), SILU)
+            nc.vector.tensor_tensor(h_bf[e][:, half * HALF:(half + 1) * HALF, :], b[:].rearrange("p t n -> p n t"), s[:], MULT)
+
+        def quantise_hidden(e):
+            codes = keep.tile([P, C], U32, name="h_codes%d" % e, align_bytes=64)
+            scales = keep.tile([P, C], U8, name="h_scales%d" % e, align_bytes=64)
+            quantise(codes[:], scales[:], h_bf[e][:].rearrange("p n t -> p (n t)"))
+            h_mx[e] = (codes, scales)
+
+        def second_layer(pair):
+            bank = psum.tile([P, 2, C], F32, name="y_bank", bufs=2)
+            for i in range(2):
+                e = 2 * pair + i
+                codes, scales = w2_mx[e // W2_GROUP]
+                wcols = slice((e % W2_GROUP) * N, (e % W2_GROUP + 1) * N)
+                nc.tensor.matmul_mx(out=bank[:, i, :], lhsT=codes[:, wcols].bitcast(FP8X4), lhsT_scale=scales[:, wcols],
+                                    rhs=h_mx[e][0][:].bitcast(FP8X4), rhs_scale=h_mx[e][1][:], start=True, stop=True)
+            nc.scalar.activation(y_slots[:, 2 * pair * C:2 * (pair + 1) * C], bank[:].rearrange("p i c -> p (i c)"), COPY)
+
+        q1, q3, g2 = {}, {}, {}
+        def gathers_after(label):
+            for g in range(E):
+                if GATHER_AFTER[g] == label:
+                    gather_tokens(g)
+
+        gathers_after(None)
+        for e in range(E + 1):
+            if e < E:
+                g1 = round_first(w1, "w1", e, V_W1[e])
+                q1[e] = quantise_weights(g1)
+            if e == E:
+                g2[0] = round_second(0)
+            if e >= 1:
+                hidden_half(e - 1, 0)
+            if e < E:
+                g3 = round_first(w3, "w3", e, V_W3[e])
+            if e >= 1:
+                hidden_half(e - 1, 1)
+            if e == E:
+                g2[1] = round_second(1)
+            if e < E:
+                q3[e] = quantise_weights(g3)
+            if e >= 1:
+                quantise_hidden(e - 1)
+            gathers_after(("w1", e))
+            gathers_after(("w3", e))
+        pairs = E // W2_GROUP
+        for g in range(pairs):
+            if g + 2 < pairs:
+                g2[g + 2] = round_second(g + 2)
+            codes = keep.tile([P, W2_GROUP * N], U32, name="w2_codes%d" % g, align_bytes=64)
+            scales = keep.tile([P, W2_GROUP * N], U8, name="w2_scales%d" % g, align_bytes=64)
+            quantise(codes[:], scales[:], g2[g][:])
+            w2_mx[g] = (codes, scales)
+            second_layer(g)
+
+        for name, src in (("pos1", pos1), ("pos2", pos2), ("pos3", pos3)):
+            lists[name] = keep.tile([P, T // LIST_ROWS], U16, name=name + "_list")
+            nc.sync.dma_start(lists[name][:], src)
+        gate_rows = gate.rearrange("r n t -> n r t")
+        first = 0
+        pending = None
+        for ci, width in enumerate(OUT_CHUNKS):
+            cols = slice(first, first + width)
+            gates = ring_tile([P, TOP, width], ("gate", ci))
+            nc.sync.dma_start(gates[:], gate_rows[:, :, cols])
+            terms = []
+            for r, name in enumerate(("pos1", "pos2", "pos3")):
+                term = tail_pool.tile([P, width], F32, name="term%d" % r)
+                part = lists[name][:, first // LIST_ROWS:(first + width) // LIST_ROWS]
+                nc.vector.tensor_tensor(term[:], y_slots[:].indirect(part), gates[:, r, :], MULT)
+                terms.append(term)
+                if r == 0 and pending is not None:
+                    finish(nc, tail_pool, out, *pending)
+            both = tail_pool.tile([P, width], F32, name="both")
+            nc.vector.tensor_tensor(both[:], terms[0][:], terms[1][:], ADD)
+            pending = (both, terms[2], cols, width)
+            first += width
+        finish(nc, tail_pool, out, *pending)
+
+
+def finish(nc, pool, out, both, third, cols, width):
+    total = pool.tile([P, width], F32, name="total")
+    nc.vector.tensor_tensor(total[:], both[:], third[:], ADD)
+    nc.sync.dma_start(out[:, cols], total[:])

@@ -1,6 +1,7 @@
 from contextlib import ExitStack
 
 import concourse.mybir as mybir
+from concourse.masks import make_identity
 
 K, T, E, C, H, N = 512, 2048, 8, 256, 512, 128
 TOP = 3
@@ -21,226 +22,243 @@ ADD = mybir.AluOpType.add
 
 P = 128
 PACK = 4
+RUN = 4
 LIST_ROWS = 16
 X_CHUNK = 512
 HALF = 128
-W2_GROUP = 2
-GATHER_EXPERTS = 1
+PAIR = 2
+ALIGN = 64
+
 RING = 16
-SLOT_BYTES = 8192
+PLACE_BYTES = 8192
+SILU_AT = (0, 2048)
+CODES_AT = 4096
+SCALES_AT = 6144
+
+X_ON_VECTOR = 80
+W3_ON_VECTOR = [64, 96, 96, 96, 96, 128, 128, 96]
 GATHER_AFTER = [None, None, None, ("w1", 0), ("w3", 0), ("w1", 2), ("w1", 3), ("w1", 4)]
-SILU_AFTER = [("w1", e + 1) for e in range(E - 1)] + [None]
-V_W1 = [0, 0, 0, 0, 0, 0, 0, 0]
-V_W3 = [64, 96, 96, 96, 96, 128, 128, 64]
-V_X = 288
-V_W2 = [0, 0, 32, 32]
-OUT_CHUNKS = [512, 512, 512, 256, 256]
+OUT_CHUNKS = [512, 512, 256, 384, 256, 128]
+SUMS_ON_TENSOR = 3
 
 
 def tile_moe_ecr_glu_silu_kernel(tc, xT, w1, w3, w2, gate, offs, pos1, pos2, pos3, out):
     nc = tc.nc
     with ExitStack() as ctx:
         keep = ctx.enter_context(tc.tile_pool(name="keep", bufs=1))
-        raw_pool = ctx.enter_context(tc.tile_pool(name="raw", bufs=1))
-        bf_pool = ctx.enter_context(tc.tile_pool(name="bf", bufs=5))
-        code_pool = ctx.enter_context(tc.tile_pool(name="code", bufs=4))
-        act_pool = ctx.enter_context(tc.tile_pool(name="act", bufs=3))
-        tail_pool = ctx.enter_context(tc.tile_pool(name="tail", bufs=2))
+        ring = ctx.enter_context(tc.tile_pool(name="ring", bufs=1))
         psum = ctx.enter_context(tc.psum_pool(name="psum", bufs=3))
-
-        x_codes = keep.tile([P, T], U32, align_bytes=64)
-        x_scales = keep.tile([P, T], U8, align_bytes=64)
-        y_slots = keep.tile([P, SLOTS + PAD], F32, align_bytes=64)
-        zeros = keep.tile([P, PAD], F32)
-        nc.gpsimd.memset(zeros[:], 0.0)
-        nc.gpsimd.memset(x_scales[:], 0)
-        nc.scalar.activation(y_slots[:, SLOTS:], zeros[:], SILU)
 
         loads = []
 
-        def ring_tile(shape, label):
-            slot = len(loads) % RING
+        def load(shape, source, label):
+            place = len(loads) % RING
             loads.append(label)
-            return raw_pool.tile(shape, F32, name="raw%d" % slot, align_bytes=64, offset=slot * SLOT_BYTES)
-
-        def tenant(pool, shape, dtype, name, after, place):
-            if after is None:
-                return pool.tile(shape, dtype, name=name, align_bytes=64)
-            slot = loads.index(after) % RING
-            return raw_pool.tile(shape, dtype, name="%s_in%d" % (name, slot), align_bytes=64,
-                                 offset=slot * SLOT_BYTES + place)
-
-        def load_rows(rows, label):
-            raw = ring_tile([P, PACK, 512], label)
-            nc.sync.dma_start(raw[:], rows)
+            raw = ring.tile(shape, F32, name="raw%d" % place, align_bytes=ALIGN, offset=place * PLACE_BYTES)
+            nc.sync.dma_start(raw[:], source)
             return raw
 
-        def round_split(dst, src, split, total):
-            if split > 0:
-                nc.vector.tensor_copy(dst[:, :split], src[:, :split])
-            if split < total:
-                nc.scalar.activation(dst[:, split:], src[:, split:], COPY)
+        def tile_after(label, shape, dtype, name, at):
+            if label is None:
+                return keep.tile(shape, dtype, name=name, align_bytes=ALIGN)
+            place = loads.index(label) % RING
+            return ring.tile(shape, dtype, name="%s_in%d" % (name, place), align_bytes=ALIGN,
+                             offset=place * PLACE_BYTES + at)
 
-        def quantise(codes, scales, grouped):
-            nc.vector.quantize_mx(out=codes.bitcast(FP8X4), scales=scales, in_=grouped)
+        def load_list(source, name):
+            offsets = keep.tile([P, T // LIST_ROWS], U16, name=name)
+            nc.sync.dma_start(offsets[:], source)
+            return offsets
 
-        x_rows = xT.rearrange("(p j) t -> p j t", j=PACK)
-        x_raw = []
-        lists = {}
-        for c in range(T // X_CHUNK):
-            x_raw.append(load_rows(x_rows[:, :, c * X_CHUNK:(c + 1) * X_CHUNK], ("x", c)))
-            if c == 0:
-                lists["offs"] = keep.tile([P, SLOTS // LIST_ROWS], U16, name="offs_list")
-                nc.sync.dma_start(lists["offs"][:], offs)
-        x_bf = []
-        for c in range(T // X_CHUNK):
-            grouped = bf_pool.tile([P, 512 * PACK], BF16, name="grouped", align_bytes=64)
-            round_split(grouped[:].rearrange("p (c i j) -> p c j i", i=4, j=PACK),
-                        x_raw[c][:].rearrange("p j (c i) -> p c j i", i=4), V_X // 4, X_CHUNK // 4)
-            x_bf.append(grouped)
-            if c > 0:
-                cols = slice((c - 1) * X_CHUNK, c * X_CHUNK)
-                quantise(x_codes[:, cols], x_scales[:, cols], x_bf[c - 1][:])
-        cols = slice(T - X_CHUNK, T)
-        quantise(x_codes[:, cols], x_scales[:, cols], x_bf[-1][:])
+        def entries(offsets, first, count):
+            return offsets[:, first // LIST_ROWS:(first + count) // LIST_ROWS]
 
-        slot_codes, slot_scales = {}, {}
+        y_slots = keep.tile([P, SLOTS + PAD], F32, align_bytes=ALIGN)
+        identity = keep.tile([P, P], F32)
+        with ExitStack() as experts:
+            rounded = experts.enter_context(tc.tile_pool(name="rounded", bufs=6))
+            packed = experts.enter_context(tc.tile_pool(name="packed", bufs=4))
+            hidden = experts.enter_context(tc.tile_pool(name="hidden", bufs=3))
+            run_experts(nc, keep, rounded, packed, hidden, psum, load, tile_after, load_list, entries,
+                        xT, w1, w3, w2, offs, y_slots, identity)
+        tail = ctx.enter_context(tc.tile_pool(name="tail", bufs=len(OUT_CHUNKS)))
+        lists = [load_list(pos, name) for pos, name in ((pos1, "pos1"), (pos2, "pos2"), (pos3, "pos3"))]
+        combine(nc, tail, psum, load, entries, lists, gate, y_slots, identity, out)
 
-        def gather_tokens(g):
-            width = GATHER_EXPERTS * C
-            part = lists["offs"][:, g * width // LIST_ROWS:(g + 1) * width // LIST_ROWS]
-            codes = tenant(keep, [P, width], U32, "slot_codes%d" % g, GATHER_AFTER[g], 4096 + 1024 * (g % 2))
-            scales = tenant(keep, [P, width], U8, "slot_scales%d" % g, GATHER_AFTER[g], 6144 + 256 * (g % 2))
-            nc.vector.tensor_copy(codes[:], x_codes[:].indirect(part))
-            nc.vector.tensor_copy(scales[:], x_scales[:].indirect(part))
-            slot_codes[g], slot_scales[g] = codes, scales
 
-        def round_first(w, label, e, split):
-            raw = load_rows(w[e].rearrange("(p j) h -> p j h", j=PACK), (label, e))
-            grouped = bf_pool.tile([P, 512 * PACK], BF16, name="grouped", align_bytes=64)
-            round_split(grouped[:].rearrange("p (t m j) -> p m j t", t=PACK, j=PACK),
-                        raw[:].rearrange("p j (m t) -> p m j t", t=PACK), split, P)
-            return grouped
+def round_shared(nc, dst, src, on_vector):
+    if on_vector > 0:
+        nc.vector.tensor_copy(dst[:, :on_vector], src[:, :on_vector])
+    if on_vector < src.shape[1]:
+        nc.scalar.activation(dst[:, on_vector:], src[:, on_vector:], COPY)
 
-        def quantise_weights(grouped):
-            codes = code_pool.tile([P, 512], U32, name="w_codes", align_bytes=64)
-            scales = code_pool.tile([P, 512], U8, name="w_scales", align_bytes=64)
-            quantise(codes[:], scales[:], grouped[:])
-            return codes, scales
 
-        def round_second(g):
-            raw = ring_tile([P, W2_GROUP, PACK, N], ("w2", g))
-            nc.sync.dma_start(raw[:].rearrange("p e j n -> p e (j n)"),
-                              w2[g * W2_GROUP:(g + 1) * W2_GROUP].rearrange("e (p j) n -> p e (j n)", j=PACK))
-            grouped = bf_pool.tile([P, W2_GROUP * N * PACK], BF16, name="grouped", align_bytes=64)
-            view = grouped[:].rearrange("p (e c i j) -> p e c j i", e=W2_GROUP, i=4, j=PACK)
-            for e in range(W2_GROUP):
-                split = min(max(V_W2[g] - e * N // 4, 0), N // 4)
-                round_split(view[:, e], raw[:, e].rearrange("p j (c i) -> p c j i", i=4), split, N // 4)
-            return grouped
+def quantise(nc, codes, scales, values):
+    nc.vector.quantize_mx(out=codes.bitcast(FP8X4), scales=scales, in_=values)
 
-        def project(name, weights, e, half):
-            codes, scales = weights
-            g, first = divmod(e * C + half * HALF, GATHER_EXPERTS * C)
-            cols = slice(first, first + HALF)
-            bank = psum.tile([P, PACK, HALF], F32, name=name)
-            for t in range(PACK):
-                wcols = slice(t * P, (t + 1) * P)
-                nc.tensor.matmul_mx(out=bank[:, t, :], lhsT=codes[:, wcols].bitcast(FP8X4), lhsT_scale=scales[:, wcols],
-                                    rhs=slot_codes[g][:, cols].bitcast(FP8X4), rhs_scale=slot_scales[g][:, cols],
-                                    start=True, stop=True)
-            return bank
 
-        h_bf, h_mx, w2_mx = {}, {}, {}
+def multiply(nc, acc, weights, weight_cols, moving, moving_cols):
+    nc.tensor.matmul_mx(out=acc, lhsT=weights[0][:, weight_cols].bitcast(FP8X4), lhsT_scale=weights[1][:, weight_cols],
+                        rhs=moving[0][:, moving_cols].bitcast(FP8X4), rhs_scale=moving[1][:, moving_cols],
+                        start=True, stop=True)
 
-        def hidden_half(e, half):
-            if half == 0:
-                h_bf[e] = act_pool.tile([P, C, PACK], BF16, name="h", align_bytes=64)
-            a = project("a_bank", q1[e], e, half)
-            b = project("b_bank", q3[e], e, half)
-            s = tenant(keep, [P, HALF, PACK], F32, "silu%d" % half, SILU_AFTER[e], 2048 * half)
-            nc.scalar.activation(s[:], a[:].rearrange("p t n -> p n t"), SILU)
-            nc.vector.tensor_tensor(h_bf[e][:, half * HALF:(half + 1) * HALF, :], b[:].rearrange("p t n -> p n t"), s[:], MULT)
 
-        def quantise_hidden(e):
-            codes = keep.tile([P, C], U32, name="h_codes%d" % e, align_bytes=64)
-            scales = keep.tile([P, C], U8, name="h_scales%d" % e, align_bytes=64)
-            quantise(codes[:], scales[:], h_bf[e][:].rearrange("p n t -> p (n t)"))
-            h_mx[e] = (codes, scales)
+def run_experts(nc, keep, rounded, packed, hidden, psum, load, tile_after, load_list, entries,
+                xT, w1, w3, w2, offs, y_slots, identity):
+    x_codes = keep.tile([P, T], U32, align_bytes=ALIGN)
+    x_scales = keep.tile([P, T], U8, align_bytes=ALIGN)
+    zeros = keep.tile([P, PAD], F32)
+    nc.gpsimd.memset(zeros[:], 0.0)
+    nc.gpsimd.memset(x_scales[:], 0)
+    nc.scalar.activation(y_slots[:, SLOTS:], zeros[:], SILU)
+    make_identity(nc, identity[:])
 
-        def second_layer(pair):
-            bank = psum.tile([P, 2, C], F32, name="y_bank", bufs=2)
-            for i in range(2):
-                e = 2 * pair + i
-                codes, scales = w2_mx[e // W2_GROUP]
-                wcols = slice((e % W2_GROUP) * N, (e % W2_GROUP + 1) * N)
-                nc.tensor.matmul_mx(out=bank[:, i, :], lhsT=codes[:, wcols].bitcast(FP8X4), lhsT_scale=scales[:, wcols],
-                                    rhs=h_mx[e][0][:].bitcast(FP8X4), rhs_scale=h_mx[e][1][:], start=True, stop=True)
-            nc.scalar.activation(y_slots[:, 2 * pair * C:2 * (pair + 1) * C], bank[:].rearrange("p i c -> p (i c)"), COPY)
+    x_rows = xT.rearrange("(p j) t -> p j t", j=PACK)
+    x_raw = [load([P, PACK, X_CHUNK], x_rows[:, :, 0:X_CHUNK], ("x", 0))]
+    slot_tokens = load_list(offs, "offs")
+    for first in range(X_CHUNK, T, X_CHUNK):
+        x_raw.append(load([P, PACK, X_CHUNK], x_rows[:, :, first:first + X_CHUNK], ("x", first)))
+    for c, raw in enumerate(x_raw):
+        values = rounded.tile([P, X_CHUNK * PACK], BF16, name="values", align_bytes=ALIGN)
+        round_shared(nc, values[:].rearrange("p (c i j) -> p c j i", i=RUN, j=PACK),
+                     raw[:].rearrange("p j (c i) -> p c j i", i=RUN), X_ON_VECTOR)
+        tokens = slice(c * X_CHUNK, (c + 1) * X_CHUNK)
+        quantise(nc, x_codes[:, tokens], x_scales[:, tokens], values[:])
 
-        q1, q3, g2 = {}, {}, {}
-        def gathers_after(label):
-            for g in range(E):
-                if GATHER_AFTER[g] == label:
-                    gather_tokens(g)
+    slots_mx, w1_mx, w3_mx, w2_mx, h_values, h_mx = {}, {}, {}, {}, {}, {}
 
-        gathers_after(None)
-        for e in range(E + 1):
-            if e < E:
-                g1 = round_first(w1, "w1", e, V_W1[e])
-                q1[e] = quantise_weights(g1)
-            if e == E:
-                g2[0] = round_second(0)
-            if e >= 1:
-                hidden_half(e - 1, 0)
-            if e < E:
-                g3 = round_first(w3, "w3", e, V_W3[e])
-            if e >= 1:
-                hidden_half(e - 1, 1)
-            if e == E:
-                g2[1] = round_second(1)
-            if e < E:
-                q3[e] = quantise_weights(g3)
-            if e >= 1:
-                quantise_hidden(e - 1)
-            gathers_after(("w1", e))
-            gathers_after(("w3", e))
-        pairs = E // W2_GROUP
-        for g in range(pairs):
-            if g + 2 < pairs:
-                g2[g + 2] = round_second(g + 2)
-            codes = keep.tile([P, W2_GROUP * N], U32, name="w2_codes%d" % g, align_bytes=64)
-            scales = keep.tile([P, W2_GROUP * N], U8, name="w2_scales%d" % g, align_bytes=64)
-            quantise(codes[:], scales[:], g2[g][:])
-            w2_mx[g] = (codes, scales)
-            second_layer(g)
+    def gather_after(label):
+        for e in range(E):
+            if GATHER_AFTER[e] == label:
+                codes = tile_after(label, [P, C], U32, "slot_codes%d" % e, CODES_AT + 4 * C * (e % 2))
+                scales = tile_after(label, [P, C], U8, "slot_scales%d" % e, SCALES_AT + C * (e % 2))
+                nc.vector.tensor_copy(codes[:], x_codes[:].indirect(entries(slot_tokens, e * C, C)))
+                nc.vector.tensor_copy(scales[:], x_scales[:].indirect(entries(slot_tokens, e * C, C)))
+                slots_mx[e] = (codes, scales)
 
-        for name, src in (("pos1", pos1), ("pos2", pos2), ("pos3", pos3)):
-            lists[name] = keep.tile([P, T // LIST_ROWS], U16, name=name + "_list")
-            nc.sync.dma_start(lists[name][:], src)
-        gate_rows = gate.rearrange("r n t -> n r t")
-        first = 0
-        pending = None
-        for ci, width in enumerate(OUT_CHUNKS):
-            cols = slice(first, first + width)
-            gates = ring_tile([P, TOP, width], ("gate", ci))
-            nc.sync.dma_start(gates[:], gate_rows[:, :, cols])
-            terms = []
-            for r, name in enumerate(("pos1", "pos2", "pos3")):
-                term = tail_pool.tile([P, width], F32, name="term%d" % r)
-                part = lists[name][:, first // LIST_ROWS:(first + width) // LIST_ROWS]
-                nc.vector.tensor_tensor(term[:], y_slots[:].indirect(part), gates[:, r, :], MULT)
-                terms.append(term)
-                if r == 0 and pending is not None:
-                    finish(nc, tail_pool, out, *pending)
-            both = tail_pool.tile([P, width], F32, name="both")
+    def round_first_layer(w, label, e, on_vector):
+        raw = load([P, PACK, H], w[e].rearrange("(p j) h -> p j h", j=PACK), (label, e))
+        values = rounded.tile([P, H * PACK], BF16, name="values", align_bytes=ALIGN)
+        round_shared(nc, values[:].rearrange("p (t m j) -> p m j t", t=PACK, j=PACK),
+                     raw[:].rearrange("p j (m t) -> p m j t", t=PACK), on_vector)
+        return values
+
+    def quantise_first_layer(values):
+        codes = packed.tile([P, H], U32, name="w_codes", align_bytes=ALIGN)
+        scales = packed.tile([P, H], U8, name="w_scales", align_bytes=ALIGN)
+        quantise(nc, codes[:], scales[:], values[:])
+        return codes, scales
+
+    def project(name, weights, e, half):
+        bank = psum.tile([P, PACK, HALF], F32, name=name)
+        for t in range(PACK):
+            multiply(nc, bank[:, t, :], weights, slice(t * P, (t + 1) * P),
+                     slots_mx[e], slice(half * HALF, (half + 1) * HALF))
+        return bank
+
+    def hidden_half(e, half):
+        if half == 0:
+            h_values[e] = hidden.tile([P, C, PACK], BF16, name="h", align_bytes=ALIGN)
+        a = project("a_bank", w1_mx[e], e, half)
+        b = project("b_bank", w3_mx[e], e, half)
+        after = ("w1", e + 1) if e + 1 < E else None
+        silu = tile_after(after, [P, HALF, PACK], F32, "silu%d" % half, SILU_AT[half])
+        nc.scalar.activation(silu[:], a[:].rearrange("p t n -> p n t"), SILU)
+        nc.vector.tensor_tensor(h_values[e][:, half * HALF:(half + 1) * HALF, :],
+                                b[:].rearrange("p t n -> p n t"), silu[:], MULT)
+
+    def quantise_hidden(e):
+        codes = keep.tile([P, C], U32, name="h_codes%d" % e, align_bytes=ALIGN)
+        scales = keep.tile([P, C], U8, name="h_scales%d" % e, align_bytes=ALIGN)
+        quantise(nc, codes[:], scales[:], h_values[e][:].rearrange("p n t -> p (n t)"))
+        h_mx[e] = (codes, scales)
+
+    def prepare_second_layer(pair):
+        source = w2[pair * PAIR:(pair + 1) * PAIR].rearrange("e (p j) n -> p e (j n)", j=PACK)
+        raw = load([P, PAIR, PACK * N], source, ("w2", pair))
+        values = rounded.tile([P, PAIR * N * PACK], BF16, name="values", align_bytes=ALIGN)
+        dst = values[:].rearrange("p (e c i j) -> p e c j i", e=PAIR, i=RUN, j=PACK)
+        src = raw[:].rearrange("p e (j c i) -> p e c j i", j=PACK, i=RUN)
+        nc.vector.tensor_copy(dst[:, 0], src[:, 0])
+        nc.scalar.activation(dst[:, 1], src[:, 1], COPY)
+        codes = keep.tile([P, PAIR * N], U32, name="w2_codes%d" % pair, align_bytes=ALIGN)
+        scales = keep.tile([P, PAIR * N], U8, name="w2_scales%d" % pair, align_bytes=ALIGN)
+        quantise(nc, codes[:], scales[:], values[:])
+        w2_mx[pair] = (codes, scales)
+
+    def second_layer(first, count):
+        bank = psum.tile([P, count, C], F32, name="y_bank", bufs=2)
+        for i in range(count):
+            pair, member = divmod(first + i, PAIR)
+            multiply(nc, bank[:, i, :], w2_mx[pair], slice(member * N, (member + 1) * N), h_mx[first + i], slice(0, C))
+        nc.scalar.activation(y_slots[:, first * C:(first + count) * C], bank[:].rearrange("p i c -> p (i c)"), COPY)
+
+    gather_after(None)
+    for e in range(E):
+        w1_mx[e] = quantise_first_layer(round_first_layer(w1, "w1", e, 0))
+        if e >= 1:
+            hidden_half(e - 1, 0)
+        w3_values = round_first_layer(w3, "w3", e, W3_ON_VECTOR[e])
+        if e >= 1:
+            hidden_half(e - 1, 1)
+        w3_mx[e] = quantise_first_layer(w3_values)
+        if e >= 1:
+            quantise_hidden(e - 1)
+        gather_after(("w1", e))
+        gather_after(("w3", e))
+    last_pair = E // PAIR - 1
+    for pair in range(last_pair):
+        prepare_second_layer(pair)
+        second_layer(pair * PAIR, PAIR)
+    hidden_half(E - 1, 0)
+    hidden_half(E - 1, 1)
+    quantise_hidden(E - 1)
+    prepare_second_layer(last_pair)
+    for e in range(last_pair * PAIR, E):
+        second_layer(e, 1)
+
+
+def combine(nc, tail, psum, load, entries, lists, gate, y_slots, identity, out):
+    gate_rows = gate.rearrange("r n t -> n r t")
+
+    def add_third(both, third, tokens, width):
+        total = tail.tile([P, width], F32, name="total")
+        nc.vector.tensor_tensor(total[:], both[:], third[:], ADD)
+        nc.sync.dma_start(out[:, tokens], total[:])
+
+    def add_in_psum(terms, tokens, width):
+        blocks = width // P
+        summed = psum.tile([P, blocks, P], F32, name="a_bank")
+        for b in range(blocks):
+            for step, term in enumerate(reversed(terms)):
+                nc.tensor.matmul(summed[:, b, :], term[:, b * P:(b + 1) * P], identity[:],
+                                 start=(step == 0), stop=(step == TOP - 1), is_transpose=True)
+        turned = tail.tile([P, blocks, P], F32, name="partial")
+        nc.scalar.activation(turned[:], summed[:], COPY)
+        back = psum.tile([P, blocks, P], F32, name="b_bank")
+        for b in range(blocks):
+            nc.tensor.transpose(back[:, b, :], turned[:, b, :], identity[:])
+        total = tail.tile([P, width], F32, name="total")
+        nc.scalar.activation(total[:], back[:].rearrange("p b t -> p (b t)"), COPY)
+        nc.sync.dma_start(out[:, tokens], total[:])
+
+    first = 0
+    waiting = None
+    for c, width in enumerate(OUT_CHUNKS):
+        tokens = slice(first, first + width)
+        gates = load([P, TOP, width], gate_rows[:, :, tokens], ("gate", c))
+        terms = []
+        for r in range(TOP):
+            term = tail.tile([P, width], F32, name="term%d" % r)
+            nc.vector.tensor_tensor(term[:], y_slots[:].indirect(entries(lists[r], first, width)), gates[:, r, :], MULT)
+            terms.append(term)
+            if r == 0 and waiting is not None:
+                add_third(*waiting)
+        if c < SUMS_ON_TENSOR:
+            add_in_psum(terms, tokens, width)
+        else:
+            both = tail.tile([P, width], F32, name="partial")
             nc.vector.tensor_tensor(both[:], terms[0][:], terms[1][:], ADD)
-            pending = (both, terms[2], cols, width)
-            first += width
-        finish(nc, tail_pool, out, *pending)
-
-
-def finish(nc, pool, out, both, third, cols, width):
-    total = pool.tile([P, width], F32, name="total")
-    nc.vector.tensor_tensor(total[:], both[:], third[:], ADD)
-    nc.sync.dma_start(out[:, cols], total[:])
+            waiting = (both, terms[2], tokens, width)
+        first += width
+    add_third(*waiting)

from contextlib import ExitStack

import concourse.mybir as mybir
from concourse.masks import make_identity

K, T, E, C, H, N = 512, 2048, 8, 256, 512, 128
TOP = 3
PAD = 64
SLOTS = E * C
FLOPS = 2 * SLOTS * (2 * K * H + H * N)

F32 = mybir.dt.float32
BF16 = mybir.dt.bfloat16
U32 = mybir.dt.uint32
U16 = mybir.dt.uint16
U8 = mybir.dt.uint8
FP8X4 = mybir.dt.float8_e4m3fn_x4
COPY = mybir.ActivationFunctionType.Copy
SILU = mybir.ActivationFunctionType.Silu
MULT = mybir.AluOpType.mult
ADD = mybir.AluOpType.add

P = 128
PACK = 4
RUN = 4
LIST_ROWS = 16
X_CHUNK = 512
HALF = 128
PAIR = 2
ALIGN = 64

RING = 16
PLACE_BYTES = 8192
SILU_AT = (0, 2048)
CODES_AT = 4096
SCALES_AT = 6144

X_ON_VECTOR = 80
W3_ON_VECTOR = [64, 96, 96, 96, 96, 128, 128, 96]
GATHER_AFTER = [None, None, None, ("w1", 0), ("w3", 0), ("w1", 2), ("w1", 3), ("w1", 4)]
OUT_CHUNKS = [512, 512, 256, 384, 256, 128]
SUMS_ON_TENSOR = 3


def tile_moe_ecr_glu_silu_kernel(tc, xT, w1, w3, w2, gate, offs, pos1, pos2, pos3, out):
    nc = tc.nc
    with ExitStack() as ctx:
        keep = ctx.enter_context(tc.tile_pool(name="keep", bufs=1))
        ring = ctx.enter_context(tc.tile_pool(name="ring", bufs=1))
        psum = ctx.enter_context(tc.psum_pool(name="psum", bufs=3))

        loads = []

        def load(shape, source, label):
            place = len(loads) % RING
            loads.append(label)
            raw = ring.tile(shape, F32, name="raw%d" % place, align_bytes=ALIGN, offset=place * PLACE_BYTES)
            nc.sync.dma_start(raw[:], source)
            return raw

        def tile_after(label, shape, dtype, name, at):
            if label is None:
                return keep.tile(shape, dtype, name=name, align_bytes=ALIGN)
            place = loads.index(label) % RING
            return ring.tile(shape, dtype, name="%s_in%d" % (name, place), align_bytes=ALIGN,
                             offset=place * PLACE_BYTES + at)

        def load_list(source, name):
            offsets = keep.tile([P, T // LIST_ROWS], U16, name=name)
            nc.sync.dma_start(offsets[:], source)
            return offsets

        def entries(offsets, first, count):
            return offsets[:, first // LIST_ROWS:(first + count) // LIST_ROWS]

        y_slots = keep.tile([P, SLOTS + PAD], F32, align_bytes=ALIGN)
        identity = keep.tile([P, P], F32)
        with ExitStack() as experts:
            rounded = experts.enter_context(tc.tile_pool(name="rounded", bufs=6))
            packed = experts.enter_context(tc.tile_pool(name="packed", bufs=4))
            hidden = experts.enter_context(tc.tile_pool(name="hidden", bufs=3))
            run_experts(nc, keep, rounded, packed, hidden, psum, load, tile_after, load_list, entries,
                        xT, w1, w3, w2, offs, y_slots, identity)
        tail = ctx.enter_context(tc.tile_pool(name="tail", bufs=len(OUT_CHUNKS)))
        lists = [load_list(pos, name) for pos, name in ((pos1, "pos1"), (pos2, "pos2"), (pos3, "pos3"))]
        combine(nc, tail, psum, load, entries, lists, gate, y_slots, identity, out)


def round_shared(nc, dst, src, on_vector):
    if on_vector > 0:
        nc.vector.tensor_copy(dst[:, :on_vector], src[:, :on_vector])
    if on_vector < src.shape[1]:
        nc.scalar.activation(dst[:, on_vector:], src[:, on_vector:], COPY)


def quantise(nc, codes, scales, values):
    nc.vector.quantize_mx(out=codes.bitcast(FP8X4), scales=scales, in_=values)


def multiply(nc, acc, weights, weight_cols, moving, moving_cols):
    nc.tensor.matmul_mx(out=acc, lhsT=weights[0][:, weight_cols].bitcast(FP8X4), lhsT_scale=weights[1][:, weight_cols],
                        rhs=moving[0][:, moving_cols].bitcast(FP8X4), rhs_scale=moving[1][:, moving_cols],
                        start=True, stop=True)


def run_experts(nc, keep, rounded, packed, hidden, psum, load, tile_after, load_list, entries,
                xT, w1, w3, w2, offs, y_slots, identity):
    x_codes = keep.tile([P, T], U32, align_bytes=ALIGN)
    x_scales = keep.tile([P, T], U8, align_bytes=ALIGN)
    zeros = keep.tile([P, PAD], F32)
    nc.gpsimd.memset(zeros[:], 0.0)
    nc.gpsimd.memset(x_scales[:], 0)
    nc.scalar.activation(y_slots[:, SLOTS:], zeros[:], SILU)
    make_identity(nc, identity[:])

    x_rows = xT.rearrange("(p j) t -> p j t", j=PACK)
    x_raw = [load([P, PACK, X_CHUNK], x_rows[:, :, 0:X_CHUNK], ("x", 0))]
    slot_tokens = load_list(offs, "offs")
    for first in range(X_CHUNK, T, X_CHUNK):
        x_raw.append(load([P, PACK, X_CHUNK], x_rows[:, :, first:first + X_CHUNK], ("x", first)))
    for c, raw in enumerate(x_raw):
        values = rounded.tile([P, X_CHUNK * PACK], BF16, name="values", align_bytes=ALIGN)
        round_shared(nc, values[:].rearrange("p (c i j) -> p c j i", i=RUN, j=PACK),
                     raw[:].rearrange("p j (c i) -> p c j i", i=RUN), X_ON_VECTOR)
        tokens = slice(c * X_CHUNK, (c + 1) * X_CHUNK)
        quantise(nc, x_codes[:, tokens], x_scales[:, tokens], values[:])

    slots_mx, w1_mx, w3_mx, w2_mx, h_values, h_mx = {}, {}, {}, {}, {}, {}

    def gather_after(label):
        for e in range(E):
            if GATHER_AFTER[e] == label:
                codes = tile_after(label, [P, C], U32, "slot_codes%d" % e, CODES_AT + 4 * C * (e % 2))
                scales = tile_after(label, [P, C], U8, "slot_scales%d" % e, SCALES_AT + C * (e % 2))
                nc.vector.tensor_copy(codes[:], x_codes[:].indirect(entries(slot_tokens, e * C, C)))
                nc.vector.tensor_copy(scales[:], x_scales[:].indirect(entries(slot_tokens, e * C, C)))
                slots_mx[e] = (codes, scales)

    def round_first_layer(w, label, e, on_vector):
        raw = load([P, PACK, H], w[e].rearrange("(p j) h -> p j h", j=PACK), (label, e))
        values = rounded.tile([P, H * PACK], BF16, name="values", align_bytes=ALIGN)
        round_shared(nc, values[:].rearrange("p (t m j) -> p m j t", t=PACK, j=PACK),
                     raw[:].rearrange("p j (m t) -> p m j t", t=PACK), on_vector)
        return values

    def quantise_first_layer(values):
        codes = packed.tile([P, H], U32, name="w_codes", align_bytes=ALIGN)
        scales = packed.tile([P, H], U8, name="w_scales", align_bytes=ALIGN)
        quantise(nc, codes[:], scales[:], values[:])
        return codes, scales

    def project(name, weights, e, half):
        bank = psum.tile([P, PACK, HALF], F32, name=name)
        for t in range(PACK):
            multiply(nc, bank[:, t, :], weights, slice(t * P, (t + 1) * P),
                     slots_mx[e], slice(half * HALF, (half + 1) * HALF))
        return bank

    def hidden_half(e, half):
        if half == 0:
            h_values[e] = hidden.tile([P, C, PACK], BF16, name="h", align_bytes=ALIGN)
        a = project("a_bank", w1_mx[e], e, half)
        b = project("b_bank", w3_mx[e], e, half)
        after = ("w1", e + 1) if e + 1 < E else None
        silu = tile_after(after, [P, HALF, PACK], F32, "silu%d" % half, SILU_AT[half])
        nc.scalar.activation(silu[:], a[:].rearrange("p t n -> p n t"), SILU)
        nc.vector.tensor_tensor(h_values[e][:, half * HALF:(half + 1) * HALF, :],
                                b[:].rearrange("p t n -> p n t"), silu[:], MULT)

    def quantise_hidden(e):
        codes = keep.tile([P, C], U32, name="h_codes%d" % e, align_bytes=ALIGN)
        scales = keep.tile([P, C], U8, name="h_scales%d" % e, align_bytes=ALIGN)
        quantise(nc, codes[:], scales[:], h_values[e][:].rearrange("p n t -> p (n t)"))
        h_mx[e] = (codes, scales)

    def prepare_second_layer(pair):
        source = w2[pair * PAIR:(pair + 1) * PAIR].rearrange("e (p j) n -> p e (j n)", j=PACK)
        raw = load([P, PAIR, PACK * N], source, ("w2", pair))
        values = rounded.tile([P, PAIR * N * PACK], BF16, name="values", align_bytes=ALIGN)
        dst = values[:].rearrange("p (e c i j) -> p e c j i", e=PAIR, i=RUN, j=PACK)
        src = raw[:].rearrange("p e (j c i) -> p e c j i", j=PACK, i=RUN)
        nc.vector.tensor_copy(dst[:, 0], src[:, 0])
        nc.scalar.activation(dst[:, 1], src[:, 1], COPY)
        codes = keep.tile([P, PAIR * N], U32, name="w2_codes%d" % pair, align_bytes=ALIGN)
        scales = keep.tile([P, PAIR * N], U8, name="w2_scales%d" % pair, align_bytes=ALIGN)
        quantise(nc, codes[:], scales[:], values[:])
        w2_mx[pair] = (codes, scales)

    def second_layer(first, count):
        bank = psum.tile([P, count, C], F32, name="y_bank", bufs=2)
        for i in range(count):
            pair, member = divmod(first + i, PAIR)
            multiply(nc, bank[:, i, :], w2_mx[pair], slice(member * N, (member + 1) * N), h_mx[first + i], slice(0, C))
        nc.scalar.activation(y_slots[:, first * C:(first + count) * C], bank[:].rearrange("p i c -> p (i c)"), COPY)

    gather_after(None)
    for e in range(E):
        w1_mx[e] = quantise_first_layer(round_first_layer(w1, "w1", e, 0))
        if e >= 1:
            hidden_half(e - 1, 0)
        w3_values = round_first_layer(w3, "w3", e, W3_ON_VECTOR[e])
        if e >= 1:
            hidden_half(e - 1, 1)
        w3_mx[e] = quantise_first_layer(w3_values)
        if e >= 1:
            quantise_hidden(e - 1)
        gather_after(("w1", e))
        gather_after(("w3", e))
    last_pair = E // PAIR - 1
    for pair in range(last_pair):
        prepare_second_layer(pair)
        second_layer(pair * PAIR, PAIR)
    hidden_half(E - 1, 0)
    hidden_half(E - 1, 1)
    quantise_hidden(E - 1)
    prepare_second_layer(last_pair)
    for e in range(last_pair * PAIR, E):
        second_layer(e, 1)


def combine(nc, tail, psum, load, entries, lists, gate, y_slots, identity, out):
    gate_rows = gate.rearrange("r n t -> n r t")

    def add_third(both, third, tokens, width):
        total = tail.tile([P, width], F32, name="total")
        nc.vector.tensor_tensor(total[:], both[:], third[:], ADD)
        nc.sync.dma_start(out[:, tokens], total[:])

    def add_in_psum(terms, tokens, width):
        blocks = width // P
        summed = psum.tile([P, blocks, P], F32, name="a_bank")
        for b in range(blocks):
            for step, term in enumerate(reversed(terms)):
                nc.tensor.matmul(summed[:, b, :], term[:, b * P:(b + 1) * P], identity[:],
                                 start=(step == 0), stop=(step == TOP - 1), is_transpose=True)
        turned = tail.tile([P, blocks, P], F32, name="partial")
        nc.scalar.activation(turned[:], summed[:], COPY)
        back = psum.tile([P, blocks, P], F32, name="b_bank")
        for b in range(blocks):
            nc.tensor.transpose(back[:, b, :], turned[:, b, :], identity[:])
        total = tail.tile([P, width], F32, name="total")
        nc.scalar.activation(total[:], back[:].rearrange("p b t -> p (b t)"), COPY)
        nc.sync.dma_start(out[:, tokens], total[:])

    first = 0
    waiting = None
    for c, width in enumerate(OUT_CHUNKS):
        tokens = slice(first, first + width)
        gates = load([P, TOP, width], gate_rows[:, :, tokens], ("gate", c))
        terms = []
        for r in range(TOP):
            term = tail.tile([P, width], F32, name="term%d" % r)
            nc.vector.tensor_tensor(term[:], y_slots[:].indirect(entries(lists[r], first, width)), gates[:, r, :], MULT)
            terms.append(term)
            if r == 0 and waiting is not None:
                add_third(*waiting)
        if c < SUMS_ON_TENSOR:
            add_in_psum(terms, tokens, width)
        else:
            both = tail.tile([P, width], F32, name="partial")
            nc.vector.tensor_tensor(both[:], terms[0][:], terms[1][:], ADD)
            waiting = (both, terms[2], tokens, width)
        first += width
    add_third(*waiting)
